import numpy as np, ml_dtypes
CORES = [88,96,104,112,120,216,224,232,240,248]
N = 10
KB, QP = 1, 512
MEM = [0,5,6]
def setup_inputs(rng):
    return {"q": rng.standard_normal((N, 128, QP), dtype=np.float32).astype(ml_dtypes.bfloat16), "k": rng.standard_normal((N, 128, KB * 128), dtype=np.float32).astype(ml_dtypes.bfloat16), "v": rng.standard_normal((N, 128, KB * 128), dtype=np.float32).astype(ml_dtypes.bfloat16)}
def setup_inputs_big(rng):
    d = setup_inputs(rng)
    for k in ("q", "k", "v"): d[k] = (d[k].astype(np.float32) * 1024.0).astype(d[k].dtype)
    return d
def setup_inputs_small(rng):
    d = setup_inputs(rng)
    for k in ("q", "k", "v"): d[k] = (d[k].astype(np.float32) * (1 / 1024.0)).astype(d[k].dtype)
    return d
def setup_inputs_apart(rng):
    d = setup_inputs(rng)
    f = (10.0 ** rng.permutation(np.linspace(-1.5, 1.5, N))).astype(np.float32).reshape(N, 1, 1)
    for k in ("q", "k", "v"): d[k] = (d[k].astype(np.float32) * f).astype(d[k].dtype)
    return d
def reference(q, k, v):
    Q, K, V = q.astype(np.float64), k.astype(np.float64), v.astype(np.float64)
    y = np.zeros((N, 128, QP))
    for r in range(N):
        for j in MEM:
            for b in range(KB):
                S = np.maximum(K[j][:, 128 * b:128 * b + 128].T @ Q[r], 0.0)
                y[r] += V[j][:, 128 * b:128 * b + 128].T @ S
    return {"y": y.astype(ml_dtypes.bfloat16 if q.dtype != np.float64 else np.float64)}

@@ -1,0 +1,196 @@
+from concourse.bass import DstId, RemoteDMATransfer
+from concourse.mybir import AluOpType
+
+NSIM = 256
+NM = 3
+F = 128
+KV = 2 * F
+QP = 512
+NCH = 2
+CW = QP // NCH
+NSB = 2 * NCH
+
+N_FEED = 8
+N_DIRECT = 8
+N_RELAY = 8
+
+SCRATCH = {
+    "kvd": ("dram", [F, KV], "bfloat16"),
+    "land": ("sbuf", [F, NM * KV], "bfloat16"),
+    "qs": ("sbuf", [F, QP], "bfloat16"),
+    "zero": ("sbuf", [F, CW], "float32"),
+    "ssb": ("sbuf", [F, NM * QP], "bfloat16"),
+    "ysb": ("sbuf", [F, QP], "bfloat16"),
+}
+for _b in range(NSB):
+    SCRATCH["sps%d" % _b] = ("psum", [F, 512], "float32")
+for _c in range(NCH):
+    SCRATCH["ops%d" % _c] = ("psum", [F, 512], "float32")
+
+SEMAPHORES = ["ld", "qld", "z", "fed", "sent"]
+SEMAPHORES += ["arr%d" % m for m in range(NM)]
+SEMAPHORES += ["s%d_%d" % (m, c) for m in range(NM) for c in range(NCH)]
+SEMAPHORES += ["r%d_%d" % (m, c) for m in range(NM) for c in range(NCH)]
+SEMAPHORES += ["o%d" % c for c in range(NCH)]
+SEMAPHORES += ["cp%d" % c for c in range(NCH)]
+SEMAPHORES += ["st%d" % c for c in range(NCH)]
+
+
+def _take(mask, n):
+    out, b = 0, 0
+    while n > 0 and (mask >> b):
+        if (mask >> b) & 1:
+            out |= 1 << b
+            n -= 1
+        b += 1
+    return out
+
+
+def _count(mask):
+    return bin(mask).count("1")
+
+
+def _common(topo, src, dsts):
+    m = topo.mask(src, dsts[0])
+    for d in dsts[1:]:
+        m &= topo.mask(src, d)
+    return m
+
+
+def _plan(T, topo):
+    cores = list(T.cores)
+    n = len(cores)
+    plan = []
+    inload = {}
+
+    def port(src, d):
+        return ("mate" if topo.mates(src, d) else "switch", topo.host(d), topo.chip(d), topo.die(src))
+
+    for j in T.tables["MEM"]:
+        s = cores[j]
+        dests = [cores[(j + i) % n] for i in range(1, n)]
+        direct = [d for d in dests if topo.may_write(s, d)]
+        cross = [d for d in dests if not topo.may_write(s, d)]
+        for d in direct:
+            inload[port(s, d)] = inload.get(port(s, d), 0) + 1
+        plan.append({"src": s, "direct": direct, "cross": cross})
+    for P in plan:
+        s, cross = P["src"], P["cross"]
+        owners = [c for c in range(NSIM) if c != s and topo.host(c) == topo.host(s) and topo.chip(c) == topo.chip(s)
+                  and all(topo.may_write(c, d) for d in cross)]
+        cap = -(-len(cross) // len(owners))
+        jobs = {h: [] for h in owners}
+        order = sorted(cross, key=lambda d: -max(inload.get(port(h, d), 0) for h in owners))
+        for d in order:
+            free = [h for h in owners if len(jobs[h]) < cap]
+            h = min(free, key=lambda c: (inload.get(port(c, d), 0), len(jobs[c]), owners.index(c)))
+            jobs[h].append(d)
+            inload[port(h, d)] = inload.get(port(h, d), 0) + 1
+        P["jobs"] = {h: dl for h, dl in jobs.items() if dl}
+        P["feed"] = sorted(P["jobs"], key=lambda h: -len(P["jobs"][h]))
+        off = _common(topo, s, P["direct"])
+        on = _common(topo, s, P["feed"])
+        P["direct_mask"] = _take(off, N_DIRECT)
+        only_on = on & ~off
+        P["feed_mask"] = _take(only_on if _count(only_on) >= N_FEED else on, N_FEED)
+        P["relay_mask"] = {h: _take(_common(topo, h, dl), N_RELAY) for h, dl in P["jobs"].items()}
+    return plan
+
+
+def _send(g, topo, core, src_ap, dst_ap, dsts, mask, remote_sem, local_sem):
+    ids = []
+    for d in dsts:
+        rid, pid = topo.addr(d, core)
+        ids.append(DstId(rid=rid, pnc=pid))
+    g.remote_dma_fused([RemoteDMATransfer(dst_ids=ids, dma_engine_mask=mask, remote_sem=remote_sem,
+                                          srcs=[src_ap], dsts=[dst_ap for _ in dsts])], local_sem=local_sem)
+
+
+def rank_program(g, core, T, topo):
+    plan = _plan(T, topo)
+    sem = T.sem
+
+    def slot(m):
+        return T.land[:, m * KV:(m + 1) * KV]
+
+    for m, P in enumerate(plan):
+        if core in P["jobs"]:
+            g.wait_ge(sem.fed, _count(P["feed_mask"]))
+            mask = P["relay_mask"][core]
+            _send(g, topo, core, T.kvd[:], slot(m), P["jobs"][core], mask, sem["arr%d" % m], sem.sent)
+            g.wait_ge(sem.sent, _count(mask))
+            return
+    if T.rank_of(core) is None:
+        return
+
+    mine = [m for m, P in enumerate(plan) if P["src"] == core]
+    if mine:
+        g.sync.dma_start(T.kvd[:, 0:F], T.k[:, :]).then_inc(sem.ld, 16)
+        g.scalar.dma_start(T.kvd[:, F:KV], T.v[:, :]).then_inc(sem.ld, 16)
+    g.sync.dma_start(T.qs[:, :], T.q[:, :]).then_inc(sem.qld, 16)
+    g.vector.memset(T.zero[:, :], 0.0).then_inc(sem.z, 1)
+
+    need = {}
+    when = {}
+    for m, P in enumerate(plan):
+        if P["src"] == core:
+            need[m], when[m] = 32, (0, 0)
+        elif core in P["direct"]:
+            need[m], when[m] = _count(P["direct_mask"]), (1, P["direct"].index(core))
+        else:
+            h = [c for c, dl in P["jobs"].items() if core in dl][0]
+            need[m], when[m] = _count(P["relay_mask"][h]), (2, P["jobs"][h].index(core))
+
+    if mine:
+        m = mine[0]
+        P = plan[m]
+        g.scalar.dma_start(T.land[:, m * KV:m * KV + F], T.k[:, :]).then_inc(sem["arr%d" % m], 16)
+        g.scalar.dma_start(T.land[:, m * KV + F:(m + 1) * KV], T.v[:, :]).then_inc(sem["arr%d" % m], 16)
+        g.wait_ge(sem.ld, 32)
+        _send(g, topo, core, T.kvd[:], T.kvd[:], P["feed"], P["feed_mask"], sem.fed, sem.sent)
+        _send(g, topo, core, T.kvd[:], slot(m), P["direct"], P["direct_mask"], sem["arr%d" % m], sem.sent)
+
+    order = sorted(range(len(plan)), key=lambda m: when[m])
+    te, ve = g.tensor, g.vector
+    te.wait_ge(sem.qld, 16)
+    ve.wait_ge(sem.z, 1)
+    last = len(order) - 1
+
+    def s_stage(i):
+        m = order[i]
+        te.wait_ge(sem["arr%d" % m], need[m])
+        for c in range(NCH):
+            sp = T["sps%d" % ((i % 2) * NCH + c)]
+            te.matmul(sp[:, 0:CW], T.land[:, m * KV:m * KV + F], T.qs[:, c * CW:(c + 1) * CW],
+                      True, True).then_inc(sem["s%d_%d" % (m, c)], 1)
+            ve.wait_ge(sem["s%d_%d" % (m, c)], 1)
+            ve.tensor_tensor(T.ssb[:, m * QP + c * CW:m * QP + (c + 1) * CW], sp[:, 0:CW], T.zero[:, :],
+                             AluOpType.max).then_inc(sem["r%d_%d" % (m, c)], 1)
+
+    def o_stage(i):
+        m = order[i]
+        for c in range(NCH):
+            te.wait_ge(sem["r%d_%d" % (m, c)], 1)
+            te.matmul(T["ops%d" % c][:, 0:CW], T.land[:, m * KV + F:(m + 1) * KV],
+                      T.ssb[:, m * QP + c * CW:m * QP + (c + 1) * CW],
+                      i == 0, i == last).then_inc(sem["o%d" % c], 1)
+
+    if when[order[last]][0] == when[order[last - 1]][0]:
+        steps = [x for i in range(last - 1) for x in ((s_stage, i), (o_stage, i))]
+        steps += [(s_stage, last - 1), (s_stage, last), (o_stage, last - 1), (o_stage, last)]
+    else:
+        steps = [x for i in range(last + 1) for x in ((s_stage, i), (o_stage, i))]
+    for fn, i in steps:
+        fn(i)
+
+    for c in range(NCH):
+        q = g.sync if c % 2 == 0 else g.scalar
+        ve.wait_ge(sem["o%d" % c], len(order))
+        ve.tensor_copy(T.ysb[:, c * CW:(c + 1) * CW], T["ops%d" % c][:, 0:CW]).then_inc(sem["cp%d" % c], 1)
+        q.wait_ge(sem["cp%d" % c], 1)
+        q.dma_start(T.y[:, c * CW:(c + 1) * CW], T.ysb[:, c * CW:(c + 1) * CW]).then_inc(sem["st%d" % c], 16)
+        q.wait_ge(sem["st%d" % c], 16)
+
+    if mine:
+        P = plan[mine[0]]
+        g.wait_ge(sem.sent, _count(P["feed_mask"]) + _count(P["direct_mask"]))

@@ -15,7 +15,8 @@ N_DIRECT = 8
 N_RELAY = 8
 
 SCRATCH = {
-    "kvd": ("dram", [F, KV], "bfloat16"),
+    "kd": ("dram", [F, F], "bfloat16"),
+    "vd": ("dram", [F, F], "bfloat16"),
     "land": ("sbuf", [F, NM * KV], "bfloat16"),
     "qs": ("sbuf", [F, QP], "bfloat16"),
     "zero": ("sbuf", [F, CW], "float32"),
@@ -27,8 +28,10 @@ for _b in range(NSB):
 for _c in range(NCH):
     SCRATCH["ops%d" % _c] = ("psum", [F, 512], "float32")
 
-SEMAPHORES = ["ld", "qld", "z", "fed", "sent"]
+SEMAPHORES = ["ldk", "ldv", "qld", "z", "fedk", "fedv", "sent"]
 SEMAPHORES += ["arr%d" % m for m in range(NM)]
+SEMAPHORES += ["ak%d" % m for m in range(NM)]
+SEMAPHORES += ["av%d" % m for m in range(NM)]
 SEMAPHORES += ["s%d_%d" % (m, c) for m in range(NM) for c in range(NCH)]
 SEMAPHORES += ["r%d_%d" % (m, c) for m in range(NM) for c in range(NCH)]
 SEMAPHORES += ["o%d" % c for c in range(NCH)]
@@ -110,45 +113,62 @@ def rank_program(g, core, T, topo):
     plan = _plan(T, topo)
     sem = T.sem
 
+    def kslot(m):
+        return T.land[:, m * KV:m * KV + F]
+
+    def vslot(m):
+        return T.land[:, m * KV + F:(m + 1) * KV]
+
     def slot(m):
         return T.land[:, m * KV:(m + 1) * KV]
 
     for m, P in enumerate(plan):
         if core in P["jobs"]:
-            g.wait_ge(sem.fed, _count(P["feed_mask"]))
+            nf = _count(P["feed_mask"])
             mask = P["relay_mask"][core]
-            _send(g, topo, core, T.kvd[:], slot(m), P["jobs"][core], mask, sem["arr%d" % m], sem.sent)
-            g.wait_ge(sem.sent, _count(mask))
+            g.wait_ge(sem.fedk, nf)
+            _send(g, topo, core, T.kd[:], kslot(m), P["jobs"][core], mask, sem["ak%d" % m], sem.sent)
+            g.wait_ge(sem.fedv, nf)
+            _send(g, topo, core, T.vd[:], vslot(m), P["jobs"][core], mask, sem["av%d" % m], sem.sent)
+            g.wait_ge(sem.sent, 2 * _count(mask))
             return
     if T.rank_of(core) is None:
         return
 
     mine = [m for m, P in enumerate(plan) if P["src"] == core]
     if mine:
-        g.sync.dma_start(T.kvd[:, 0:F], T.k[:, :]).then_inc(sem.ld, 16)
-        g.scalar.dma_start(T.kvd[:, F:KV], T.v[:, :]).then_inc(sem.ld, 16)
+        g.sync.dma_start(T.kd[:, :], T.k[:, :]).then_inc(sem.ldk, 16)
+        g.scalar.dma_start(T.vd[:, :], T.v[:, :]).then_inc(sem.ldv, 16)
+        m = mine[0]
+        g.sync.dma_start(kslot(m), T.k[:, :]).then_inc(sem["arr%d" % m], 16)
+        g.scalar.dma_start(vslot(m), T.v[:, :]).then_inc(sem["arr%d" % m], 16)
     g.sync.dma_start(T.qs[:, :], T.q[:, :]).then_inc(sem.qld, 16)
     g.vector.memset(T.zero[:, :], 0.0).then_inc(sem.z, 1)
 
-    need = {}
+    kwait = {}
+    vwait = {}
     when = {}
     for m, P in enumerate(plan):
         if P["src"] == core:
-            need[m], when[m] = 32, (0, 0)
+            kwait[m], vwait[m], when[m] = ("arr%d" % m, 32), None, (0, 0)
         elif core in P["direct"]:
-            need[m], when[m] = _count(P["direct_mask"]), (1, P["direct"].index(core))
+            kwait[m], vwait[m] = ("arr%d" % m, _count(P["direct_mask"])), None
+            when[m] = (1, P["direct"].index(core))
         else:
             h = [c for c, dl in P["jobs"].items() if core in dl][0]
-            need[m], when[m] = _count(P["relay_mask"][h]), (2, P["jobs"][h].index(core))
+            nr = _count(P["relay_mask"][h])
+            kwait[m], vwait[m] = ("ak%d" % m, nr), ("av%d" % m, nr)
+            when[m] = (2, P["feed"].index(h) + 2 * P["jobs"][h].index(core))
 
     if mine:
         m = mine[0]
         P = plan[m]
-        g.scalar.dma_start(T.land[:, m * KV:m * KV + F], T.k[:, :]).then_inc(sem["arr%d" % m], 16)
-        g.scalar.dma_start(T.land[:, m * KV + F:(m + 1) * KV], T.v[:, :]).then_inc(sem["arr%d" % m], 16)
-        g.wait_ge(sem.ld, 32)
-        _send(g, topo, core, T.kvd[:], T.kvd[:], P["feed"], P["feed_mask"], sem.fed, sem.sent)
-        _send(g, topo, core, T.kvd[:], slot(m), P["direct"], P["direct_mask"], sem["arr%d" % m], sem.sent)
+        g.wait_ge(sem.ldk, 16)
+        _send(g, topo, core, T.kd[:], T.kd[:], P["feed"], P["feed_mask"], sem.fedk, sem.sent)
+        g.wait_ge(sem.ldv, 16)
+        _send(g, topo, core, T.vd[:], T.vd[:], P["feed"], P["feed_mask"], sem.fedv, sem.sent)
+        g.wait_ge(sem["arr%d" % m], 32)
+        _send(g, topo, core, slot(m), slot(m), P["direct"], P["direct_mask"], sem["arr%d" % m], sem.sent)
 
     order = sorted(range(len(plan)), key=lambda m: when[m])
     te, ve = g.tensor, g.vector
@@ -158,10 +178,10 @@ def rank_program(g, core, T, topo):
 
     def s_stage(i):
         m = order[i]
-        te.wait_ge(sem["arr%d" % m], need[m])
+        te.wait_ge(sem[kwait[m][0]], kwait[m][1])
         for c in range(NCH):
             sp = T["sps%d" % ((i % 2) * NCH + c)]
-            te.matmul(sp[:, 0:CW], T.land[:, m * KV:m * KV + F], T.qs[:, c * CW:(c + 1) * CW],
+            te.matmul(sp[:, 0:CW], kslot(m), T.qs[:, c * CW:(c + 1) * CW],
                       True, True).then_inc(sem["s%d_%d" % (m, c)], 1)
             ve.wait_ge(sem["s%d_%d" % (m, c)], 1)
             ve.tensor_tensor(T.ssb[:, m * QP + c * CW:m * QP + (c + 1) * CW], sp[:, 0:CW], T.zero[:, :],
@@ -169,9 +189,11 @@ def rank_program(g, core, T, topo):
 
     def o_stage(i):
         m = order[i]
+        if vwait[m] is not None:
+            te.wait_ge(sem[vwait[m][0]], vwait[m][1])
         for c in range(NCH):
             te.wait_ge(sem["r%d_%d" % (m, c)], 1)
-            te.matmul(T["ops%d" % c][:, 0:CW], T.land[:, m * KV + F:(m + 1) * KV],
+            te.matmul(T["ops%d" % c][:, 0:CW], vslot(m),
                       T.ssb[:, m * QP + c * CW:m * QP + (c + 1) * CW],
                       i == 0, i == last).then_inc(sem["o%d" % c], 1)
 
@@ -193,4 +215,4 @@ def rank_program(g, core, T, topo):
 
     if mine:
         P = plan[mine[0]]
-        g.wait_ge(sem.sent, _count(P["feed_mask"]) + _count(P["direct_mask"]))
+        g.wait_ge(sem.sent, 2 * _count(P["feed_mask"]) + _count(P["direct_mask"]))

@@ -9,6 +9,9 @@ QP = 512
 NCH = 2
 CW = QP // NCH
 NSB = 2 * NCH
+NO = 4
+OW = QP // NO
+KEEP = 4
 
 N_FEED = 8
 N_DIRECT = 8
@@ -25,7 +28,7 @@ SCRATCH = {
 }
 for _b in range(NSB):
     SCRATCH["sps%d" % _b] = ("psum", [F, 512], "float32")
-for _c in range(NCH):
+for _c in range(NO):
     SCRATCH["ops%d" % _c] = ("psum", [F, 512], "float32")
 
 SEMAPHORES = ["ldk", "ldv", "qld", "z", "fedk", "fedv", "sent"]
@@ -34,7 +37,7 @@ SEMAPHORES += ["ak%d" % m for m in range(NM)]
 SEMAPHORES += ["av%d" % m for m in range(NM)]
 SEMAPHORES += ["s%d_%d" % (m, c) for m in range(NM) for c in range(NCH)]
 SEMAPHORES += ["r%d_%d" % (m, c) for m in range(NM) for c in range(NCH)]
-SEMAPHORES += ["o%d" % c for c in range(NCH)]
+SEMAPHORES += ["o%d" % c for c in range(NO)]
 SEMAPHORES += ["cp%d" % c for c in range(NCH)]
 SEMAPHORES += ["st%d" % c for c in range(NCH)]
 
@@ -65,6 +68,7 @@ def _plan(T, topo):
     n = len(cores)
     plan = []
     inload = {}
+    mem = [cores[j] for j in T.tables["MEM"]]
 
     def port(src, d):
         return ("mate" if topo.mates(src, d) else "switch", topo.host(d), topo.chip(d), topo.die(src))
@@ -72,25 +76,30 @@ def _plan(T, topo):
     for j in T.tables["MEM"]:
         s = cores[j]
         dests = [cores[(j + i) % n] for i in range(1, n)]
-        direct = [d for d in dests if topo.may_write(s, d)]
+        same = [d for d in dests if topo.may_write(s, d)]
         cross = [d for d in dests if not topo.may_write(s, d)]
+        direct, extra = same[:KEEP], same[KEEP:]
         for d in direct:
             inload[port(s, d)] = inload.get(port(s, d), 0) + 1
-        plan.append({"src": s, "direct": direct, "cross": cross})
+        plan.append({"src": s, "direct": direct, "extra": extra, "cross": cross})
     for P in plan:
         s, cross = P["src"], P["cross"]
-        owners = [c for c in range(NSIM) if c != s and topo.host(c) == topo.host(s) and topo.chip(c) == topo.chip(s)
-                  and all(topo.may_write(c, d) for d in cross)]
+        chipmates = [c for c in range(NSIM) if c != s and topo.host(c) == topo.host(s) and topo.chip(c) == topo.chip(s)]
+        owners = [c for c in chipmates if all(topo.may_write(c, d) for d in cross)]
         cap = -(-len(cross) // len(owners))
         jobs = {h: [] for h in owners}
-        order = sorted(cross, key=lambda d: -max(inload.get(port(h, d), 0) for h in owners))
+        order = sorted(cross, key=lambda d: (d in mem, -max(inload.get(port(h, d), 0) for h in owners)))
         for d in order:
             free = [h for h in owners if len(jobs[h]) < cap]
-            h = min(free, key=lambda c: (inload.get(port(c, d), 0), len(jobs[c]), owners.index(c)))
+            h = min(free, key=lambda c: (len(jobs[c]), inload.get(port(c, d), 0), owners.index(c)))
             jobs[h].append(d)
             inload[port(h, d)] = inload.get(port(h, d), 0) + 1
         P["jobs"] = {h: dl for h, dl in jobs.items() if dl}
         P["feed"] = sorted(P["jobs"], key=lambda h: -len(P["jobs"][h]))
+        spare = sorted([c for c in chipmates if c not in P["jobs"]], key=lambda c: (topo.die(c) == topo.die(s), c))
+        for d, h in zip(P["extra"], spare):
+            P["jobs"][h] = [d]
+            P["feed"].append(h)
         off = _common(topo, s, P["direct"])
         on = _common(topo, s, P["feed"])
         P["direct_mask"] = _take(off, N_DIRECT)
@@ -191,11 +200,12 @@ def rank_program(g, core, T, topo):
         m = order[i]
         if vwait[m] is not None:
             te.wait_ge(sem[vwait[m][0]], vwait[m][1])
-        for c in range(NCH):
-            te.wait_ge(sem["r%d_%d" % (m, c)], 1)
-            te.matmul(T["ops%d" % c][:, 0:CW], vslot(m),
-                      T.ssb[:, m * QP + c * CW:m * QP + (c + 1) * CW],
-                      i == 0, i == last).then_inc(sem["o%d" % c], 1)
+        for j in range(NO):
+            if (j * OW) % CW == 0:
+                te.wait_ge(sem["r%d_%d" % (m, (j * OW) // CW)], 1)
+            te.matmul(T["ops%d" % j][:, 0:OW], vslot(m),
+                      T.ssb[:, m * QP + j * OW:m * QP + (j + 1) * OW],
+                      i == 0, i == last).then_inc(sem["o%d" % j], 1)
 
     if when[order[last]][0] == when[order[last - 1]][0]:
         steps = [x for i in range(last - 1) for x in ((s_stage, i), (o_stage, i))]
@@ -205,11 +215,13 @@ def rank_program(g, core, T, topo):
     for fn, i in steps:
         fn(i)
 
+    per = NO // NCH
     for c in range(NCH):
         q = g.sync if c % 2 == 0 else g.scalar
-        ve.wait_ge(sem["o%d" % c], len(order))
-        ve.tensor_copy(T.ysb[:, c * CW:(c + 1) * CW], T["ops%d" % c][:, 0:CW]).then_inc(sem["cp%d" % c], 1)
-        q.wait_ge(sem["cp%d" % c], 1)
+        for j in range(c * per, (c + 1) * per):
+            ve.wait_ge(sem["o%d" % j], len(order))
+            ve.tensor_copy(T.ysb[:, j * OW:(j + 1) * OW], T["ops%d" % j][:, 0:OW]).then_inc(sem["cp%d" % c], 1)
+        q.wait_ge(sem["cp%d" % c], per)
         q.dma_start(T.y[:, c * CW:(c + 1) * CW], T.ysb[:, c * CW:(c + 1) * CW]).then_inc(sem["st%d" % c], 16)
         q.wait_ge(sem["st%d" % c], 16)
 

from concourse.bass import DstId, RemoteDMATransfer
from concourse.mybir import AluOpType

NSIM = 256
NM = 3
F = 128
KV = 2 * F
QP = 512
NCH = 2
CW = QP // NCH
NSB = 2 * NCH
NO = 4
OW = QP // NO
KEEP = 4

N_FEED = 8
N_DIRECT = 8
N_RELAY = 8

SCRATCH = {
    "kd": ("dram", [F, F], "bfloat16"),
    "vd": ("dram", [F, F], "bfloat16"),
    "land": ("sbuf", [F, NM * KV], "bfloat16"),
    "qs": ("sbuf", [F, QP], "bfloat16"),
    "zero": ("sbuf", [F, CW], "float32"),
    "ssb": ("sbuf", [F, NM * QP], "bfloat16"),
    "ysb": ("sbuf", [F, QP], "bfloat16"),
}
for _b in range(NSB):
    SCRATCH["sps%d" % _b] = ("psum", [F, 512], "float32")
for _c in range(NO):
    SCRATCH["ops%d" % _c] = ("psum", [F, 512], "float32")

SEMAPHORES = ["ldk", "ldv", "qld", "z", "fedk", "fedv", "sent"]
SEMAPHORES += ["arr%d" % m for m in range(NM)]
SEMAPHORES += ["ak%d" % m for m in range(NM)]
SEMAPHORES += ["av%d" % m for m in range(NM)]
SEMAPHORES += ["s%d_%d" % (m, c) for m in range(NM) for c in range(NCH)]
SEMAPHORES += ["r%d_%d" % (m, c) for m in range(NM) for c in range(NCH)]
SEMAPHORES += ["o%d" % c for c in range(NO)]
SEMAPHORES += ["cp%d" % c for c in range(NCH)]
SEMAPHORES += ["st%d" % c for c in range(NCH)]


def _take(mask, n):
    out, b = 0, 0
    while n > 0 and (mask >> b):
        if (mask >> b) & 1:
            out |= 1 << b
            n -= 1
        b += 1
    return out


def _count(mask):
    return bin(mask).count("1")


def _common(topo, src, dsts):
    m = topo.mask(src, dsts[0])
    for d in dsts[1:]:
        m &= topo.mask(src, d)
    return m


def _plan(T, topo):
    cores = list(T.cores)
    n = len(cores)
    plan = []
    inload = {}
    mem = [cores[j] for j in T.tables["MEM"]]

    def port(src, d):
        return ("mate" if topo.mates(src, d) else "switch", topo.host(d), topo.chip(d), topo.die(src))

    for j in T.tables["MEM"]:
        s = cores[j]
        dests = [cores[(j + i) % n] for i in range(1, n)]
        same = [d for d in dests if topo.may_write(s, d)]
        cross = [d for d in dests if not topo.may_write(s, d)]
        direct, extra = same[:KEEP], same[KEEP:]
        for d in direct:
            inload[port(s, d)] = inload.get(port(s, d), 0) + 1
        plan.append({"src": s, "direct": direct, "extra": extra, "cross": cross})
    for P in plan:
        s, cross = P["src"], P["cross"]
        chipmates = [c for c in range(NSIM) if c != s and topo.host(c) == topo.host(s) and topo.chip(c) == topo.chip(s)]
        owners = [c for c in chipmates if all(topo.may_write(c, d) for d in cross)]
        cap = -(-len(cross) // len(owners))
        jobs = {h: [] for h in owners}
        order = sorted(cross, key=lambda d: (d in mem, -max(inload.get(port(h, d), 0) for h in owners)))
        for d in order:
            free = [h for h in owners if len(jobs[h]) < cap]
            h = min(free, key=lambda c: (len(jobs[c]), inload.get(port(c, d), 0), owners.index(c)))
            jobs[h].append(d)
            inload[port(h, d)] = inload.get(port(h, d), 0) + 1
        P["jobs"] = {h: dl for h, dl in jobs.items() if dl}
        P["feed"] = sorted(P["jobs"], key=lambda h: -len(P["jobs"][h]))
        spare = sorted([c for c in chipmates if c not in P["jobs"]], key=lambda c: (topo.die(c) == topo.die(s), c))
        for d, h in zip(P["extra"], spare):
            P["jobs"][h] = [d]
            P["feed"].append(h)
        off = _common(topo, s, P["direct"])
        on = _common(topo, s, P["feed"])
        P["direct_mask"] = _take(off, N_DIRECT)
        only_on = on & ~off
        P["feed_mask"] = _take(only_on if _count(only_on) >= N_FEED else on, N_FEED)
        P["relay_mask"] = {h: _take(_common(topo, h, dl), N_RELAY) for h, dl in P["jobs"].items()}
    return plan


def _send(g, topo, core, src_ap, dst_ap, dsts, mask, remote_sem, local_sem):
    ids = []
    for d in dsts:
        rid, pid = topo.addr(d, core)
        ids.append(DstId(rid=rid, pnc=pid))
    g.remote_dma_fused([RemoteDMATransfer(dst_ids=ids, dma_engine_mask=mask, remote_sem=remote_sem,
                                          srcs=[src_ap], dsts=[dst_ap for _ in dsts])], local_sem=local_sem)


def rank_program(g, core, T, topo):
    plan = _plan(T, topo)
    sem = T.sem

    def kslot(m):
        return T.land[:, m * KV:m * KV + F]

    def vslot(m):
        return T.land[:, m * KV + F:(m + 1) * KV]

    def slot(m):
        return T.land[:, m * KV:(m + 1) * KV]

    for m, P in enumerate(plan):
        if core in P["jobs"]:
            nf = _count(P["feed_mask"])
            mask = P["relay_mask"][core]
            g.wait_ge(sem.fedk, nf)
            _send(g, topo, core, T.kd[:], kslot(m), P["jobs"][core], mask, sem["ak%d" % m], sem.sent)
            g.wait_ge(sem.fedv, nf)
            _send(g, topo, core, T.vd[:], vslot(m), P["jobs"][core], mask, sem["av%d" % m], sem.sent)
            g.wait_ge(sem.sent, 2 * _count(mask))
            return
    if T.rank_of(core) is None:
        return

    mine = [m for m, P in enumerate(plan) if P["src"] == core]
    if mine:
        g.sync.dma_start(T.kd[:, :], T.k[:, :]).then_inc(sem.ldk, 16)
        g.scalar.dma_start(T.vd[:, :], T.v[:, :]).then_inc(sem.ldv, 16)
        m = mine[0]
        g.sync.dma_start(kslot(m), T.k[:, :]).then_inc(sem["arr%d" % m], 16)
        g.scalar.dma_start(vslot(m), T.v[:, :]).then_inc(sem["arr%d" % m], 16)
    g.sync.dma_start(T.qs[:, :], T.q[:, :]).then_inc(sem.qld, 16)
    g.vector.memset(T.zero[:, :], 0.0).then_inc(sem.z, 1)

    kwait = {}
    vwait = {}
    when = {}
    for m, P in enumerate(plan):
        if P["src"] == core:
            kwait[m], vwait[m], when[m] = ("arr%d" % m, 32), None, (0, 0)
        elif core in P["direct"]:
            kwait[m], vwait[m] = ("arr%d" % m, _count(P["direct_mask"])), None
            when[m] = (1, P["direct"].index(core))
        else:
            h = [c for c, dl in P["jobs"].items() if core in dl][0]
            nr = _count(P["relay_mask"][h])
            kwait[m], vwait[m] = ("ak%d" % m, nr), ("av%d" % m, nr)
            when[m] = (2, P["feed"].index(h) + 2 * P["jobs"][h].index(core))

    if mine:
        m = mine[0]
        P = plan[m]
        g.wait_ge(sem.ldk, 16)
        _send(g, topo, core, T.kd[:], T.kd[:], P["feed"], P["feed_mask"], sem.fedk, sem.sent)
        g.wait_ge(sem.ldv, 16)
        _send(g, topo, core, T.vd[:], T.vd[:], P["feed"], P["feed_mask"], sem.fedv, sem.sent)
        g.wait_ge(sem["arr%d" % m], 32)
        _send(g, topo, core, slot(m), slot(m), P["direct"], P["direct_mask"], sem["arr%d" % m], sem.sent)

    order = sorted(range(len(plan)), key=lambda m: when[m])
    te, ve = g.tensor, g.vector
    te.wait_ge(sem.qld, 16)
    ve.wait_ge(sem.z, 1)
    last = len(order) - 1

    def s_stage(i):
        m = order[i]
        te.wait_ge(sem[kwait[m][0]], kwait[m][1])
        for c in range(NCH):
            sp = T["sps%d" % ((i % 2) * NCH + c)]
            te.matmul(sp[:, 0:CW], kslot(m), T.qs[:, c * CW:(c + 1) * CW],
                      True, True).then_inc(sem["s%d_%d" % (m, c)], 1)
            ve.wait_ge(sem["s%d_%d" % (m, c)], 1)
            ve.tensor_tensor(T.ssb[:, m * QP + c * CW:m * QP + (c + 1) * CW], sp[:, 0:CW], T.zero[:, :],
                             AluOpType.max).then_inc(sem["r%d_%d" % (m, c)], 1)

    def o_stage(i):
        m = order[i]
        if vwait[m] is not None:
            te.wait_ge(sem[vwait[m][0]], vwait[m][1])
        for j in range(NO):
            if (j * OW) % CW == 0:
                te.wait_ge(sem["r%d_%d" % (m, (j * OW) // CW)], 1)
            te.matmul(T["ops%d" % j][:, 0:OW], vslot(m),
                      T.ssb[:, m * QP + j * OW:m * QP + (j + 1) * OW],
                      i == 0, i == last).then_inc(sem["o%d" % j], 1)

    if when[order[last]][0] == when[order[last - 1]][0]:
        steps = [x for i in range(last - 1) for x in ((s_stage, i), (o_stage, i))]
        steps += [(s_stage, last - 1), (s_stage, last), (o_stage, last - 1), (o_stage, last)]
    else:
        steps = [x for i in range(last + 1) for x in ((s_stage, i), (o_stage, i))]
    for fn, i in steps:
        fn(i)

    per = NO // NCH
    for c in range(NCH):
        q = g.sync if c % 2 == 0 else g.scalar
        for j in range(c * per, (c + 1) * per):
            ve.wait_ge(sem["o%d" % j], len(order))
            ve.tensor_copy(T.ysb[:, j * OW:(j + 1) * OW], T["ops%d" % j][:, 0:OW]).then_inc(sem["cp%d" % c], 1)
        q.wait_ge(sem["cp%d" % c], per)
        q.dma_start(T.y[:, c * CW:(c + 1) * CW], T.ysb[:, c * CW:(c + 1) * CW]).then_inc(sem["st%d" % c], 16)
        q.wait_ge(sem["st%d" % c], 16)

    if mine:
        P = plan[mine[0]]
        g.wait_ge(sem.sent, 2 * _count(P["feed_mask"]) + _count(P["direct_mask"]))
